import numpy as np
import ml_dtypes


def mxq(x, axis, fmt="e4m3"):
    dtype, down = {"e4m3": (ml_dtypes.float8_e4m3fn, 7), "e5m2": (ml_dtypes.float8_e5m2, 14)}[fmt]
    v = np.moveaxis(np.asarray(x, np.float32).astype(ml_dtypes.bfloat16).astype(np.float64), axis, -1)
    blocks = v.reshape(v.shape[:-1] + (-1, 32))
    amax = np.abs(blocks).max(-1, keepdims=True)
    byte = np.maximum(np.where(amax > 0, np.frexp(amax)[1] - 1 + 127, 0) - down, 1)
    scale = np.exp2(byte - 127.0)
    codes = (blocks / scale).astype(np.float32).astype(dtype).astype(np.float64)
    return np.moveaxis((codes * scale).reshape(v.shape), -1, axis)


WIDE = False


def mx_kscale(k):
    if not WIDE:
        return np.ones(k)
    levels = np.array([10, -10, 5, -5, 0])
    if k % 512:
        return np.exp2(np.random.permutation(np.resize(levels, k // 32))).repeat(32)
    a = np.empty((k // 512, 16))
    for p in range(k // 512):
        a[p, :8] = np.random.permutation(np.resize(levels, 8))
        for g in range(8):
            far = levels[np.abs(levels - a[p, g]) >= 10]
            a[p, g + 8] = far[np.random.randint(len(far))]
    return np.exp2(a.ravel()).repeat(32)


def f64(x):
    return np.asarray(x).astype(np.float64)


def striped(idx):
    return np.tile(idx.reshape(-1, 16).T, (8, 1)).astype(np.uint16)


def unstriped(offs):
    return offs[:16].T.reshape(-1).astype(np.int64)


def pack_weight(w):
    k, n = w.shape
    w = f64(np.asarray(w, np.float32).astype(ml_dtypes.bfloat16)).reshape(k // 32, 32, n)
    amax = np.abs(w).max(1)
    byte = np.clip(np.where(amax > 0, np.frexp(amax)[1] - 1 + 127 - 7, 1), 1, 254)
    scaled = (w * np.exp2(127.0 - byte)[:, None, :]).reshape(k, n).astype(np.float32)
    words = np.ascontiguousarray(scaled.reshape(k // 512, 128, 4, n).transpose(0, 1, 3, 2)).astype(ml_dtypes.float8_e4m3fn).view(np.uint8)
    return words, np.ascontiguousarray(byte.astype(np.uint8).reshape(k // 512, 16, n))


def unpack_weight(words, scales):
    g, p, n, _ = words.shape
    vals = np.ascontiguousarray(words).view(ml_dtypes.float8_e4m3fn).astype(np.float64) * np.repeat(np.exp2(scales.astype(np.float64) - 127.0), 8, axis=1)[..., None]
    return vals.transpose(0, 1, 3, 2).reshape(g * 512, n)


K, T, S, D, N, V = 1024, 2048, 512, 4, 256, 128
P = 2 ** 7


def setup_inputs():
    n = np.random.standard_normal
    s = mx_kscale(K)[:, None]
    packed_xT = pack_weight(n((K, T)) * s)
    return {
        "x_words": packed_xT[0],
        "x_scales": packed_xT[1],
        "w1": (n((K, N)) / np.sqrt(K) / s).astype(np.float32),
        "w2": (n((K, N)) / np.sqrt(K) / s).astype(np.float32),
        "trt": (np.tile((np.random.uniform(size=S) < 0.5) * 1.0, (P, 1))).astype(np.float32),
        "cap": (np.tile(np.random.uniform(1.5, 4.0, V), (P, 1))).astype(np.float32),
        "obs": (n((N, V))).astype(np.float32),
        "offs": striped(np.random.permutation(T)[:S]),
    }


def reference(x_words, x_scales, w1, w2, trt, cap, obs, offs):
    xq = unpack_weight(x_words, x_scales)[:, unstriped(offs)]
    yn = mxq(f64(w1), 0, "e4m3").T @ xq
    yd = mxq(f64(w2), 0, "e4m3").T @ xq
    lr = f64(trt)[:1] * yn - (np.log(np.exp(yn) + 1.0)) - (f64(trt)[:1] * yd - (np.log(np.exp(yd) + 1.0)))
    lw = lr.reshape(len(lr), -1, D).sum(axis=2)
    wt = np.minimum(np.exp(lw), f64(cap)[:1])
    mw = wt.mean(axis=1, keepdims=True)
    return (wt * f64(obs)) / mw

@@ -1,0 +1,182 @@
+import math
+from contextlib import ExitStack
+
+import concourse.mybir as mybir
+from concourse.masks import make_identity
+
+K, T, S, D, N, V = 1024, 2048, 512, 4, 256, 128
+FLOPS = 2 * 2 * K * S * N
+
+F32 = mybir.dt.float32
+BF16 = mybir.dt.bfloat16
+I32 = mybir.dt.int32
+U32 = mybir.dt.uint32
+U16 = mybir.dt.uint16
+U8 = mybir.dt.uint8
+FP8X4 = mybir.dt.float8_e4m3fn_x4
+ALU = mybir.AluOpType
+ACT = mybir.ActivationFunctionType
+
+P = 128
+PACK = 4
+PASSES = K // (P * PACK)
+M_TILES = N // P
+CUT = 16.0
+
+
+def tile_picked_ymsmw_mean_p_kernel(tc, x_words, x_scales, w1, w2, trt, cap, obs, offs, out):
+    nc = tc.nc
+    with ExitStack() as ctx:
+        sb = ctx.enter_context(tc.tile_pool(name="sb", bufs=1))
+        ps = ctx.enter_context(tc.psum_pool(name="ps", bufs=1))
+
+        offsets = sb.tile([P, S // 16], U16, name="offsets")
+
+        scale_table = sb.tile([P, T], U8, name="scale_table", align_bytes=64)
+        nc.gpsimd.memset(scale_table[:, : T // 4].bitcast(I32), 0)
+        nc.vector.memset(scale_table[:, T // 4 :].bitcast(I32), 0)
+
+        def load_weights(g, o):
+            rows = sb.tile([P, PACK, N], F32, name=f"raw{g}{o}")
+            nc.sync.dma_start(rows[:], (w1, w2)[g][o * P * PACK : (o + 1) * P * PACK, :].rearrange("(p j) c -> p j c", j=PACK))
+            return rows
+
+        raw = {(0, 0): load_weights(0, 0)}
+        nc.sync.dma_start(offsets[:], offs)
+        treated = sb.tile([P, D], F32, name="treated")
+        nc.sync.dma_start(treated[:], trt[0:1, :].rearrange("a (v d) -> (a v) d", d=D))
+        for q in range(4):
+            nc.sync.dma_start(scale_table[32 * q : 32 * q + 4 * PASSES, :].bitcast(I32), x_scales[:, 4 * q : 4 * q + 4, :].bitcast(I32))
+        word_tables = []
+        for o in range(PASSES):
+            table = sb.tile([P, T], I32, name=f"word_table{o}", align_bytes=64)
+            nc.sync.dma_start(table[:], x_words[o].rearrange("p c r -> p (c r)").bitcast(I32))
+            word_tables.append(table)
+        for g, o in ((0, 1), (1, 0), (1, 1)):
+            raw[g, o] = load_weights(g, o)
+        cap_sb = sb.tile([P, V], F32, name="cap_sb")
+        nc.sync.dma_start(cap_sb[:], cap)
+        obs_sb = sb.tile([P, M_TILES, V], F32, name="obs_sb")
+        nc.sync.dma_start(obs_sb[:], obs.rearrange("(t p) v -> p t v", p=P))
+
+        sign = sb.tile([P, D], F32, name="sign")
+        nc.scalar.activation(sign[:], treated[:], ACT.Copy, scale=2.0, bias=-1.0)
+        neg_sign = sb.tile([P, D], F32, name="neg_sign")
+        nc.scalar.activation(neg_sign[:], treated[:], ACT.Copy, scale=-2.0, bias=1.0)
+        ident = sb.tile([P, P], F32, name="ident")
+        make_identity(nc, ident[:])
+
+        picked_scales = sb.tile([P, S], U8, name="picked_scales", align_bytes=64)
+        nc.vector.tensor_copy(picked_scales[:], scale_table[:].indirect(offsets[:]))
+        x_sc = sb.tile([P, S], U8, name="x_sc", align_bytes=64)
+        nc.vector.tensor_copy(x_sc[:].rearrange("p (d v) -> p v d", d=D), picked_scales[:].rearrange("p (v d) -> p v d", d=D))
+        x_codes = []
+        for o in range(PASSES):
+            codes = sb.tile([P, S], U32, name=f"x_codes{o}", align_bytes=64)
+            nc.vector.tensor_copy(codes[:].rearrange("p (d v) -> p v d", d=D), word_tables[o][:].bitcast(U32).indirect(offsets[:]))
+            x_codes.append(codes)
+
+        def interleave(engine_copy, grouped, src, c0, c1):
+            engine_copy(
+                grouped[:, c0:c1, :].rearrange("p (c i) j -> p c j i", i=4),
+                src[:, :, c0:c1].rearrange("p j (c i) -> p c j i", i=4),
+            )
+
+        def quantize(g, o, vector_cols):
+            grouped = sb.tile([P, N, PACK], BF16, name=f"grouped{g}{o}", align_bytes=64)
+            if vector_cols:
+                interleave(nc.vector.tensor_copy, grouped, raw[g, o], 0, vector_cols)
+            if vector_cols < N:
+                interleave(nc.scalar.copy, grouped, raw[g, o], vector_cols, N)
+            codes = sb.tile([P, N], U32, name=f"w_codes{g}{o}", align_bytes=64)
+            scales = sb.tile([P, N], U8, name=f"w_scales{g}{o}", align_bytes=64)
+            nc.vector.quantize_mx(out=codes[:].bitcast(FP8X4), scales=scales[:], in_=grouped[:].rearrange("p c j -> p (c j)"))
+            return codes, scales
+
+        def product_pass(banks, o, codes, scales):
+            for d in range(D):
+                cols = slice(d * V, (d + 1) * V)
+                nc.tensor.matmul_mx(
+                    out=banks[d][:],
+                    lhsT=x_codes[o][:, cols].bitcast(FP8X4),
+                    lhsT_scale=x_sc[4 * o : P, cols],
+                    rhs=codes[:].bitcast(FP8X4),
+                    rhs_scale=scales[:],
+                    start=(o == 0),
+                    stop=(o == PASSES - 1),
+                )
+
+        yn = [ps.tile([P, N], F32, name=f"yn{d}", tag=f"bank{d}") for d in range(D)]
+        yd = [ps.tile([P, N], F32, name=f"yd{d}", tag=f"bank{D + d}") for d in range(D)]
+        shares = {(0, 0): 176, (0, 1): 144, (1, 0): 192, (1, 1): N}
+        for o in range(PASSES):
+            product_pass(yn, o, *quantize(0, o, shares[0, o]))
+        for o in range(PASSES):
+            product_pass(yd, o, *quantize(1, o, shares[1, o]))
+
+        linear = []
+        factor = None
+        for d in range(D):
+            mag = sb.tile([P, N], F32, name=f"mag{d}")
+            nc.scalar.activation(mag[:], yn[d][:], ACT.Abs)
+            lin = sb.tile([P, N], F32, name=f"lin_n{d}")
+            nc.vector.tensor_scalar(lin[:], yn[d][:], sign[:, d : d + 1], 0.0, ALU.mult, ALU.min)
+            linear.append(lin)
+            th = sb.tile([P, N], F32, name=f"th{d}")
+            nc.scalar.activation(th[:], mag[:], ACT.Tanh, scale=0.5)
+            nxt = sb.tile([P, N], F32, name=f"factor_n{d}")
+            if factor is None:
+                nc.vector.tensor_scalar(nxt[:], th[:], 1.0, 0.5**D, ALU.add, ALU.mult)
+            else:
+                nc.vector.scalar_tensor_tensor(nxt[:], th[:], 1.0, factor[:], ALU.add, ALU.mult)
+            factor = nxt
+
+
+        expo = [ps.tile([P, V], F32, name=f"expo{t}", tag=f"bank{t}") for t in range(M_TILES)]
+        fact_t = [ps.tile([P, V], F32, name=f"fact_t{t}", tag=f"bank{M_TILES + t}") for t in range(M_TILES)]
+
+        def add_transposed(banks, src, start, stop):
+            for t in range(M_TILES):
+                nc.tensor.matmul(banks[t][:], src[:, t * P : (t + 1) * P], ident[:], start=start, stop=stop, is_transpose=True)
+
+        for d in range(D):
+            add_transposed(expo, linear[d], d == 0, False)
+
+        for d in range(D):
+            lin = sb.tile([P, N], F32, name=f"lin_d{d}")
+            nc.scalar.activation(lin[:], yd[d][:], ACT.Relu, scale=neg_sign[:, d : d + 1], bias=-CUT)
+            add_transposed(expo, lin, False, d == D - 1)
+            if d < D - 1:
+                odds = sb.tile([P, N], F32, name=f"odds{d}")
+                nc.scalar.activation(odds[:], yd[d][:], ACT.Exp, scale=neg_sign[:, d : d + 1])
+                inv = sb.tile([P, N], F32, name=f"inv{d}")
+                nc.vector.tensor_scalar(inv[:], odds[:], math.exp(CUT), 1.0, ALU.min, ALU.add)
+                nxt = sb.tile([P, N], F32, name=f"factor_d{d}")
+                nc.vector.tensor_tensor(nxt[:], inv[:], factor[:], ALU.mult)
+                factor = nxt
+        add_transposed(fact_t, factor, True, False)
+        for t in range(M_TILES):
+            cols = slice(t * P, (t + 1) * P)
+            odds = sb.tile([P, P], F32, name=f"last_odds{t}")
+            nc.scalar.activation(odds[:], yd[D - 1][:, cols], ACT.Exp, scale=neg_sign[:, D - 1 : D])
+            term = sb.tile([P, P], F32, name=f"last_term{t}")
+            nc.vector.scalar_tensor_tensor(term[:], odds[:], math.exp(CUT), factor[:, cols], ALU.min, ALU.mult)
+            nc.tensor.matmul(fact_t[t][:], term[:], ident[:], start=False, stop=True, is_transpose=True)
+
+        obs_v = sb.tile([P, M_TILES, V], F32, name="obs_v")
+        nc.gpsimd.tensor_scalar(obs_v[:], obs_sb[:], float(V), 0.0, ALU.mult, ALU.add)
+
+        stores = (nc.sync, nc.scalar)
+        for t in range(M_TILES):
+            grown = sb.tile([P, V], F32, name=f"grown{t}")
+            nc.scalar.activation(grown[:], expo[t][:], ACT.Exp)
+            uncut = sb.tile([P, V], F32, name=f"uncut{t}")
+            nc.vector.tensor_tensor(uncut[:], fact_t[t][:], grown[:], ALU.mult)
+            wt = sb.tile([P, V], F32, name=f"wt{t}")
+            total = sb.tile([P, 1], F32, name=f"total{t}")
+            nc.vector.scalar_tensor_tensor(wt[:], uncut[:], 1.0, cap_sb[:], ALU.mult, ALU.min, accum_out=total[:])
+            inv_total = sb.tile([P, 1], F32, name=f"inv_total{t}")
+            nc.vector.reciprocal(inv_total[:], total[:])
+            result = sb.tile([P, V], F32, name=f"result{t}")
+            nc.vector.scalar_tensor_tensor(result[:], wt[:], inv_total[:], obs_v[:, t, :], ALU.mult, ALU.mult)
+            stores[t].dma_start(out[t * P : (t + 1) * P, :], result[:])

@@ -37,7 +37,7 @@ def tile_picked_ymsmw_mean_p_kernel(tc, x_words, x_scales, w1, w2, trt, cap, obs
         nc.vector.memset(scale_table[:, T // 4 :].bitcast(I32), 0)
 
         def load_weights(g, o):
-            rows = sb.tile([P, PACK, N], F32, name=f"raw{g}{o}")
+            rows = sb.tile([P, PACK, N], F32, name=f"raw{g}{o}", tag=f"raw{g}{o}")
             nc.sync.dma_start(rows[:], (w1, w2)[g][o * P * PACK : (o + 1) * P * PACK, :].rearrange("(p j) c -> p j c", j=PACK))
             return rows
 
@@ -66,102 +66,121 @@ def tile_picked_ymsmw_mean_p_kernel(tc, x_words, x_scales, w1, w2, trt, cap, obs
         ident = sb.tile([P, P], F32, name="ident")
         make_identity(nc, ident[:])
 
+        def gather_words(o):
+            codes = sb.tile([P, S], U32, name=f"x_codes{o}", align_bytes=64)
+            nc.vector.tensor_copy(codes[:].rearrange("p (d v) -> p v d", d=D), word_tables[o][:].bitcast(U32).indirect(offsets[:]))
+            return codes
+
         picked_scales = sb.tile([P, S], U8, name="picked_scales", align_bytes=64)
         nc.vector.tensor_copy(picked_scales[:], scale_table[:].indirect(offsets[:]))
         x_sc = sb.tile([P, S], U8, name="x_sc", align_bytes=64)
         nc.vector.tensor_copy(x_sc[:].rearrange("p (d v) -> p v d", d=D), picked_scales[:].rearrange("p (v d) -> p v d", d=D))
-        x_codes = []
-        for o in range(PASSES):
-            codes = sb.tile([P, S], U32, name=f"x_codes{o}", align_bytes=64)
-            nc.vector.tensor_copy(codes[:].rearrange("p (d v) -> p v d", d=D), word_tables[o][:].bitcast(U32).indirect(offsets[:]))
-            x_codes.append(codes)
 
-        def interleave(engine_copy, grouped, src, c0, c1):
-            engine_copy(
-                grouped[:, c0:c1, :].rearrange("p (c i) j -> p c j i", i=4),
-                src[:, :, c0:c1].rearrange("p j (c i) -> p c j i", i=4),
-            )
+        x_codes = [gather_words(0)]
 
-        def quantize(g, o, vector_cols):
-            grouped = sb.tile([P, N, PACK], BF16, name=f"grouped{g}{o}", align_bytes=64)
-            if vector_cols:
-                interleave(nc.vector.tensor_copy, grouped, raw[g, o], 0, vector_cols)
-            if vector_cols < N:
-                interleave(nc.scalar.copy, grouped, raw[g, o], vector_cols, N)
-            codes = sb.tile([P, N], U32, name=f"w_codes{g}{o}", align_bytes=64)
-            scales = sb.tile([P, N], U8, name=f"w_scales{g}{o}", align_bytes=64)
+        def interleave(g, o, grouped, vector_cols):
+            for copy, c0, c1 in ((nc.vector.tensor_copy, 0, vector_cols), (nc.scalar.copy, vector_cols, N)):
+                if c0 < c1:
+                    copy(
+                        grouped[:, c0:c1, :].rearrange("p (c i) j -> p c j i", i=4),
+                        raw[g, o][:, :, c0:c1].rearrange("p j (c i) -> p c j i", i=4),
+                    )
+
+        def quantize(name, grouped, width):
+            codes = sb.tile([P, width], U32, name=f"{name}_codes", align_bytes=64)
+            scales = sb.tile([P, width], U8, name=f"{name}_scales", align_bytes=64)
             nc.vector.quantize_mx(out=codes[:].bitcast(FP8X4), scales=scales[:], in_=grouped[:].rearrange("p c j -> p (c j)"))
             return codes, scales
 
-        def product_pass(banks, o, codes, scales):
-            for d in range(D):
-                cols = slice(d * V, (d + 1) * V)
-                nc.tensor.matmul_mx(
-                    out=banks[d][:],
-                    lhsT=x_codes[o][:, cols].bitcast(FP8X4),
-                    lhsT_scale=x_sc[4 * o : P, cols],
-                    rhs=codes[:].bitcast(FP8X4),
-                    rhs_scale=scales[:],
-                    start=(o == 0),
-                    stop=(o == PASSES - 1),
-                )
+        def product(bank, d, o, codes, scales):
+            cols = slice(d * V, (d + 1) * V)
+            nc.tensor.matmul_mx(
+                out=bank[:],
+                lhsT=x_codes[o][:, cols].bitcast(FP8X4),
+                lhsT_scale=x_sc[4 * o : P, cols],
+                rhs=codes.bitcast(FP8X4),
+                rhs_scale=scales,
+                start=(o == 0),
+                stop=(o == PASSES - 1),
+            )
 
         yn = [ps.tile([P, N], F32, name=f"yn{d}", tag=f"bank{d}") for d in range(D)]
         yd = [ps.tile([P, N], F32, name=f"yd{d}", tag=f"bank{D + d}") for d in range(D)]
-        shares = {(0, 0): 176, (0, 1): 144, (1, 0): 192, (1, 1): N}
-        for o in range(PASSES):
-            product_pass(yn, o, *quantize(0, o, shares[0, o]))
-        for o in range(PASSES):
-            product_pass(yd, o, *quantize(1, o, shares[1, o]))
-
-        linear = []
-        factor = None
-        for d in range(D):
-            mag = sb.tile([P, N], F32, name=f"mag{d}")
-            nc.scalar.activation(mag[:], yn[d][:], ACT.Abs)
-            lin = sb.tile([P, N], F32, name=f"lin_n{d}")
-            nc.vector.tensor_scalar(lin[:], yn[d][:], sign[:, d : d + 1], 0.0, ALU.mult, ALU.min)
-            linear.append(lin)
-            th = sb.tile([P, N], F32, name=f"th{d}")
-            nc.scalar.activation(th[:], mag[:], ACT.Tanh, scale=0.5)
-            nxt = sb.tile([P, N], F32, name=f"factor_n{d}")
-            if factor is None:
-                nc.vector.tensor_scalar(nxt[:], th[:], 1.0, 0.5**D, ALU.add, ALU.mult)
-            else:
-                nc.vector.scalar_tensor_tensor(nxt[:], th[:], 1.0, factor[:], ALU.add, ALU.mult)
-            factor = nxt
-
+        for o, vector_cols in enumerate((176, 128)):
+            if o > 0:
+                x_codes.append(gather_words(o))
+            grouped = sb.tile([P, N, PACK], BF16, name=f"w1_grouped{o}", align_bytes=64)
+            interleave(0, o, grouped, vector_cols)
+            codes, scales = quantize(f"w1_{o}", grouped, N)
+            for d in range(D):
+                product(yn[d], d, o, codes[:], scales[:])
+        for o, vector_cols in enumerate((128, N)):
+            grouped = sb.tile([P, N, PACK], BF16, name=f"w2_grouped{o}", align_bytes=64)
+            interleave(1, o, grouped, vector_cols)
+            codes, scales = quantize(f"w2_{o}", grouped, N)
+            for d in range(D):
+                product(yd[d], d, o, codes[:], scales[:])
 
         expo = [ps.tile([P, V], F32, name=f"expo{t}", tag=f"bank{t}") for t in range(M_TILES)]
         fact_t = [ps.tile([P, V], F32, name=f"fact_t{t}", tag=f"bank{M_TILES + t}") for t in range(M_TILES)]
 
-        def add_transposed(banks, src, start, stop):
-            for t in range(M_TILES):
-                nc.tensor.matmul(banks[t][:], src[:, t * P : (t + 1) * P], ident[:], start=start, stop=stop, is_transpose=True)
+        def add_transposed(bank, src, start, stop):
+            nc.tensor.matmul(bank[:], src, ident[:], start=start, stop=stop, is_transpose=True)
 
+        def tile_cols(t):
+            return slice(t * P, (t + 1) * P)
+
+        th = []
         for d in range(D):
-            add_transposed(expo, linear[d], d == 0, False)
+            mag = sb.tile([P, N], F32, name=f"mag{d}")
+            nc.scalar.activation(mag[:], yn[d][:], ACT.Abs)
+            th.append(sb.tile([P, N], F32, name=f"th{d}"))
+            nc.scalar.activation(th[d][:], mag[:], ACT.Tanh, scale=0.5)
+            if d == 0:
+                first = sb.tile([P, N], F32, name="first")
+                nc.scalar.activation(first[:], th[0][:], ACT.Copy, scale=0.5**D, bias=0.5**D)
+
+        parts = sb.tile([P, D + 1, N], F32, name="parts", tag="raw11")
+        factor = first[:]
+        for d in range(D):
+            nc.vector.tensor_scalar(parts[:, d, :], yn[d][:], sign[:, d : d + 1], 0.0, ALU.mult, ALU.min)
+            if d > 0:
+                prod = parts[:, D, :] if d == 1 else sb.tile([P, N], F32, name=f"times_n{d}")[:]
+                nc.vector.scalar_tensor_tensor(prod, th[d][:], 1.0, factor, ALU.add, ALU.mult)
+                factor = prod
+            for t in range(M_TILES):
+                add_transposed(expo[t], parts[:, d, tile_cols(t)], d == 0, False)
+
+        odds = sb.tile([P, D, N], F32, name="odds")
+        for d in range(D):
+            nc.scalar.activation(odds[:, d, :], yd[d][:], ACT.Exp, scale=neg_sign[:, d : d + 1])
+        inv01 = sb.tile([P, 2, N], F32, name="inv01")
+        nc.vector.tensor_scalar(inv01[:], odds[:, 0:2, :], math.exp(CUT), 1.0, ALU.min, ALU.add)
+        inv2 = sb.tile([P, N], F32, name="inv2")
+        nc.vector.tensor_scalar(inv2[:], odds[:, 2, :], math.exp(CUT), 1.0, ALU.min, ALU.add)
+        pair = sb.tile([P, N], F32, name="pair")
+        nc.vector.tensor_tensor(pair[:], inv01[:, 0, :], inv01[:, 1, :], ALU.mult)
+        right = []
+        for t in range(M_TILES):
+            right.append(sb.tile([P, P], F32, name=f"right{t}"))
+            nc.vector.tensor_tensor(right[t][:], inv2[:, tile_cols(t)], factor[:, tile_cols(t)], ALU.mult)
+        most = []
+        for t in range(M_TILES):
+            most.append(sb.tile([P, P], F32, name=f"most{t}"))
+            nc.vector.tensor_tensor(most[t][:], pair[:, tile_cols(t)], right[t][:], ALU.mult)
+            add_transposed(fact_t[t], most[t][:], True, False)
+        for t in range(M_TILES):
+            term = sb.tile([P, P], F32, name=f"last_term{t}")
+            nc.vector.scalar_tensor_tensor(term[:], odds[:, D - 1, tile_cols(t)], math.exp(CUT), most[t][:], ALU.min, ALU.mult)
+            add_transposed(fact_t[t], term[:], False, True)
 
         for d in range(D):
             lin = sb.tile([P, N], F32, name=f"lin_d{d}")
-            nc.scalar.activation(lin[:], yd[d][:], ACT.Relu, scale=neg_sign[:, d : d + 1], bias=-CUT)
-            add_transposed(expo, lin, False, d == D - 1)
-            if d < D - 1:
-                odds = sb.tile([P, N], F32, name=f"odds{d}")
-                nc.scalar.activation(odds[:], yd[d][:], ACT.Exp, scale=neg_sign[:, d : d + 1])
-                inv = sb.tile([P, N], F32, name=f"inv{d}")
-                nc.vector.tensor_scalar(inv[:], odds[:], math.exp(CUT), 1.0, ALU.min, ALU.add)
-                nxt = sb.tile([P, N], F32, name=f"factor_d{d}")
-                nc.vector.tensor_tensor(nxt[:], inv[:], factor[:], ALU.mult)
-                factor = nxt
-        add_transposed(fact_t, factor, True, False)
-        for t in range(M_TILES):
-            cols = slice(t * P, (t + 1) * P)
-            odds = sb.tile([P, P], F32, name=f"last_odds{t}")
-            nc.scalar.activation(odds[:], yd[D - 1][:, cols], ACT.Exp, scale=neg_sign[:, D - 1 : D])
-            term = sb.tile([P, P], F32, name=f"last_term{t}")
-            nc.vector.scalar_tensor_tensor(term[:], odds[:], math.exp(CUT), factor[:, cols], ALU.min, ALU.mult)
-            nc.tensor.matmul(fact_t[t][:], term[:], ident[:], start=False, stop=True, is_transpose=True)
+            pieces = [slice(0, N)] if d < D - 1 else [tile_cols(t) for t in range(M_TILES)]
+            for cols in pieces:
+                nc.scalar.activation(lin[:, cols], yd[d][:, cols], ACT.Relu, scale=neg_sign[:, d : d + 1], bias=-CUT)
+            for t in range(M_TILES):
+                add_transposed(expo[t], lin[:, tile_cols(t)], False, d == D - 1)
 
         obs_v = sb.tile([P, M_TILES, V], F32, name="obs_v")
         nc.gpsimd.tensor_scalar(obs_v[:], obs_sb[:], float(V), 0.0, ALU.mult, ALU.add)

import math
from contextlib import ExitStack

import concourse.mybir as mybir
from concourse.masks import make_identity

K, T, S, D, N, V = 1024, 2048, 512, 4, 256, 128
FLOPS = 2 * 2 * K * S * N

F32 = mybir.dt.float32
BF16 = mybir.dt.bfloat16
I32 = mybir.dt.int32
U32 = mybir.dt.uint32
U16 = mybir.dt.uint16
U8 = mybir.dt.uint8
FP8X4 = mybir.dt.float8_e4m3fn_x4
ALU = mybir.AluOpType
ACT = mybir.ActivationFunctionType

P = 128
PACK = 4
PASSES = K // (P * PACK)
M_TILES = N // P
CUT = 16.0


def tile_picked_ymsmw_mean_p_kernel(tc, x_words, x_scales, w1, w2, trt, cap, obs, offs, out):
    nc = tc.nc
    with ExitStack() as ctx:
        sb = ctx.enter_context(tc.tile_pool(name="sb", bufs=1))
        ps = ctx.enter_context(tc.psum_pool(name="ps", bufs=1))

        offsets = sb.tile([P, S // 16], U16, name="offsets")

        scale_table = sb.tile([P, T], U8, name="scale_table", align_bytes=64)
        nc.gpsimd.memset(scale_table[:, : T // 4].bitcast(I32), 0)
        nc.vector.memset(scale_table[:, T // 4 :].bitcast(I32), 0)

        def load_weights(g, o):
            rows = sb.tile([P, PACK, N], F32, name=f"raw{g}{o}", tag=f"raw{g}{o}")
            nc.sync.dma_start(rows[:], (w1, w2)[g][o * P * PACK : (o + 1) * P * PACK, :].rearrange("(p j) c -> p j c", j=PACK))
            return rows

        raw = {(0, 0): load_weights(0, 0)}
        nc.sync.dma_start(offsets[:], offs)
        treated = sb.tile([P, D], F32, name="treated")
        nc.sync.dma_start(treated[:], trt[0:1, :].rearrange("a (v d) -> (a v) d", d=D))
        for q in range(4):
            nc.sync.dma_start(scale_table[32 * q : 32 * q + 4 * PASSES, :].bitcast(I32), x_scales[:, 4 * q : 4 * q + 4, :].bitcast(I32))
        word_tables = []
        for o in range(PASSES):
            table = sb.tile([P, T], I32, name=f"word_table{o}", align_bytes=64)
            nc.sync.dma_start(table[:], x_words[o].rearrange("p c r -> p (c r)").bitcast(I32))
            word_tables.append(table)
        for g, o in ((0, 1), (1, 0), (1, 1)):
            raw[g, o] = load_weights(g, o)
        cap_sb = sb.tile([P, V], F32, name="cap_sb")
        nc.sync.dma_start(cap_sb[:], cap)
        obs_sb = sb.tile([P, M_TILES, V], F32, name="obs_sb")
        nc.sync.dma_start(obs_sb[:], obs.rearrange("(t p) v -> p t v", p=P))

        sign = sb.tile([P, D], F32, name="sign")
        nc.scalar.activation(sign[:], treated[:], ACT.Copy, scale=2.0, bias=-1.0)
        neg_sign = sb.tile([P, D], F32, name="neg_sign")
        nc.scalar.activation(neg_sign[:], treated[:], ACT.Copy, scale=-2.0, bias=1.0)
        ident = sb.tile([P, P], F32, name="ident")
        make_identity(nc, ident[:])

        def gather_words(o):
            codes = sb.tile([P, S], U32, name=f"x_codes{o}", align_bytes=64)
            nc.vector.tensor_copy(codes[:].rearrange("p (d v) -> p v d", d=D), word_tables[o][:].bitcast(U32).indirect(offsets[:]))
            return codes

        picked_scales = sb.tile([P, S], U8, name="picked_scales", align_bytes=64)
        nc.vector.tensor_copy(picked_scales[:], scale_table[:].indirect(offsets[:]))
        x_sc = sb.tile([P, S], U8, name="x_sc", align_bytes=64)
        nc.vector.tensor_copy(x_sc[:].rearrange("p (d v) -> p v d", d=D), picked_scales[:].rearrange("p (v d) -> p v d", d=D))

        x_codes = [gather_words(0)]

        def interleave(g, o, grouped, vector_cols):
            for copy, c0, c1 in ((nc.vector.tensor_copy, 0, vector_cols), (nc.scalar.copy, vector_cols, N)):
                if c0 < c1:
                    copy(
                        grouped[:, c0:c1, :].rearrange("p (c i) j -> p c j i", i=4),
                        raw[g, o][:, :, c0:c1].rearrange("p j (c i) -> p c j i", i=4),
                    )

        def quantize(name, grouped, width):
            codes = sb.tile([P, width], U32, name=f"{name}_codes", align_bytes=64)
            scales = sb.tile([P, width], U8, name=f"{name}_scales", align_bytes=64)
            nc.vector.quantize_mx(out=codes[:].bitcast(FP8X4), scales=scales[:], in_=grouped[:].rearrange("p c j -> p (c j)"))
            return codes, scales

        def product(bank, d, o, codes, scales):
            cols = slice(d * V, (d + 1) * V)
            nc.tensor.matmul_mx(
                out=bank[:],
                lhsT=x_codes[o][:, cols].bitcast(FP8X4),
                lhsT_scale=x_sc[4 * o : P, cols],
                rhs=codes.bitcast(FP8X4),
                rhs_scale=scales,
                start=(o == 0),
                stop=(o == PASSES - 1),
            )

        yn = [ps.tile([P, N], F32, name=f"yn{d}", tag=f"bank{d}") for d in range(D)]
        yd = [ps.tile([P, N], F32, name=f"yd{d}", tag=f"bank{D + d}") for d in range(D)]
        for o, vector_cols in enumerate((176, 128)):
            if o > 0:
                x_codes.append(gather_words(o))
            grouped = sb.tile([P, N, PACK], BF16, name=f"w1_grouped{o}", align_bytes=64)
            interleave(0, o, grouped, vector_cols)
            codes, scales = quantize(f"w1_{o}", grouped, N)
            for d in range(D):
                product(yn[d], d, o, codes[:], scales[:])
        for o, vector_cols in enumerate((128, N)):
            grouped = sb.tile([P, N, PACK], BF16, name=f"w2_grouped{o}", align_bytes=64)
            interleave(1, o, grouped, vector_cols)
            codes, scales = quantize(f"w2_{o}", grouped, N)
            for d in range(D):
                product(yd[d], d, o, codes[:], scales[:])

        expo = [ps.tile([P, V], F32, name=f"expo{t}", tag=f"bank{t}") for t in range(M_TILES)]
        fact_t = [ps.tile([P, V], F32, name=f"fact_t{t}", tag=f"bank{M_TILES + t}") for t in range(M_TILES)]

        def add_transposed(bank, src, start, stop):
            nc.tensor.matmul(bank[:], src, ident[:], start=start, stop=stop, is_transpose=True)

        def tile_cols(t):
            return slice(t * P, (t + 1) * P)

        th = []
        for d in range(D):
            mag = sb.tile([P, N], F32, name=f"mag{d}")
            nc.scalar.activation(mag[:], yn[d][:], ACT.Abs)
            th.append(sb.tile([P, N], F32, name=f"th{d}"))
            nc.scalar.activation(th[d][:], mag[:], ACT.Tanh, scale=0.5)
            if d == 0:
                first = sb.tile([P, N], F32, name="first")
                nc.scalar.activation(first[:], th[0][:], ACT.Copy, scale=0.5**D, bias=0.5**D)

        parts = sb.tile([P, D + 1, N], F32, name="parts", tag="raw11")
        factor = first[:]
        for d in range(D):
            nc.vector.tensor_scalar(parts[:, d, :], yn[d][:], sign[:, d : d + 1], 0.0, ALU.mult, ALU.min)
            if d > 0:
                prod = parts[:, D, :] if d == 1 else sb.tile([P, N], F32, name=f"times_n{d}")[:]
                nc.vector.scalar_tensor_tensor(prod, th[d][:], 1.0, factor, ALU.add, ALU.mult)
                factor = prod
            for t in range(M_TILES):
                add_transposed(expo[t], parts[:, d, tile_cols(t)], d == 0, False)

        odds = sb.tile([P, D, N], F32, name="odds")
        for d in range(D):
            nc.scalar.activation(odds[:, d, :], yd[d][:], ACT.Exp, scale=neg_sign[:, d : d + 1])
        inv01 = sb.tile([P, 2, N], F32, name="inv01")
        nc.vector.tensor_scalar(inv01[:], odds[:, 0:2, :], math.exp(CUT), 1.0, ALU.min, ALU.add)
        inv2 = sb.tile([P, N], F32, name="inv2")
        nc.vector.tensor_scalar(inv2[:], odds[:, 2, :], math.exp(CUT), 1.0, ALU.min, ALU.add)
        pair = sb.tile([P, N], F32, name="pair")
        nc.vector.tensor_tensor(pair[:], inv01[:, 0, :], inv01[:, 1, :], ALU.mult)
        right = []
        for t in range(M_TILES):
            right.append(sb.tile([P, P], F32, name=f"right{t}"))
            nc.vector.tensor_tensor(right[t][:], inv2[:, tile_cols(t)], factor[:, tile_cols(t)], ALU.mult)
        most = []
        for t in range(M_TILES):
            most.append(sb.tile([P, P], F32, name=f"most{t}"))
            nc.vector.tensor_tensor(most[t][:], pair[:, tile_cols(t)], right[t][:], ALU.mult)
            add_transposed(fact_t[t], most[t][:], True, False)
        for t in range(M_TILES):
            term = sb.tile([P, P], F32, name=f"last_term{t}")
            nc.vector.scalar_tensor_tensor(term[:], odds[:, D - 1, tile_cols(t)], math.exp(CUT), most[t][:], ALU.min, ALU.mult)
            add_transposed(fact_t[t], term[:], False, True)

        for d in range(D):
            lin = sb.tile([P, N], F32, name=f"lin_d{d}")
            pieces = [slice(0, N)] if d < D - 1 else [tile_cols(t) for t in range(M_TILES)]
            for cols in pieces:
                nc.scalar.activation(lin[:, cols], yd[d][:, cols], ACT.Relu, scale=neg_sign[:, d : d + 1], bias=-CUT)
            for t in range(M_TILES):
                add_transposed(expo[t], lin[:, tile_cols(t)], False, d == D - 1)

        obs_v = sb.tile([P, M_TILES, V], F32, name="obs_v")
        nc.gpsimd.tensor_scalar(obs_v[:], obs_sb[:], float(V), 0.0, ALU.mult, ALU.add)

        stores = (nc.sync, nc.scalar)
        for t in range(M_TILES):
            grown = sb.tile([P, V], F32, name=f"grown{t}")
            nc.scalar.activation(grown[:], expo[t][:], ACT.Exp)
            uncut = sb.tile([P, V], F32, name=f"uncut{t}")
            nc.vector.tensor_tensor(uncut[:], fact_t[t][:], grown[:], ALU.mult)
            wt = sb.tile([P, V], F32, name=f"wt{t}")
            total = sb.tile([P, 1], F32, name=f"total{t}")
            nc.vector.scalar_tensor_tensor(wt[:], uncut[:], 1.0, cap_sb[:], ALU.mult, ALU.min, accum_out=total[:])
            inv_total = sb.tile([P, 1], F32, name=f"inv_total{t}")
            nc.vector.reciprocal(inv_total[:], total[:])
            result = sb.tile([P, V], F32, name=f"result{t}")
            nc.vector.scalar_tensor_tensor(result[:], wt[:], inv_total[:], obs_v[:, t, :], ALU.mult, ALU.mult)
            stores[t].dma_start(out[t * P : (t + 1) * P, :], result[:])
